import numpy as np
import ml_dtypes


def mxq(x, axis, fmt="e4m3"):
    dtype, down = {"e4m3": (ml_dtypes.float8_e4m3fn, 7), "e5m2": (ml_dtypes.float8_e5m2, 14)}[fmt]
    v = np.moveaxis(np.asarray(x, np.float32).astype(ml_dtypes.bfloat16).astype(np.float64), axis, -1)
    blocks = v.reshape(v.shape[:-1] + (-1, 32))
    amax = np.abs(blocks).max(-1, keepdims=True)
    byte = np.maximum(np.where(amax > 0, np.frexp(amax)[1] - 1 + 127, 0) - down, 1)
    scale = np.exp2(byte - 127.0)
    codes = (blocks / scale).astype(np.float32).astype(dtype).astype(np.float64)
    return np.moveaxis((codes * scale).reshape(v.shape), -1, axis)


WIDE = False


def mx_kscale(k):
    if not WIDE:
        return np.ones(k)
    levels = np.array([10, -10, 5, -5, 0])
    if k % 512:
        return np.exp2(np.random.permutation(np.resize(levels, k // 32))).repeat(32)
    a = np.empty((k // 512, 16))
    for p in range(k // 512):
        a[p, :8] = np.random.permutation(np.resize(levels, 8))
        for g in range(8):
            far = levels[np.abs(levels - a[p, g]) >= 10]
            a[p, g + 8] = far[np.random.randint(len(far))]
    return np.exp2(a.ravel()).repeat(32)


def f64(x):
    return np.asarray(x).astype(np.float64)


def striped(idx):
    return np.tile(np.asarray(idx).reshape(-1, 16).T, (8, 1)).astype(np.uint16)


def unstriped(offs):
    return offs[:16].T.reshape(-1).astype(np.int64)


B, N, T, D, DV, NQ = 1, 1024, 4096, 512, 256, 128


def setup_inputs():
    n = np.random.standard_normal
    idx = np.random.permutation(T)[:B * N]
    s = mx_kscale(D)[:, None]
    u = np.ones(T)
    u[idx] = mx_kscale(B * N)
    r = np.random.uniform(0.5, 2.0, T)
    rk = np.random.uniform(0.5, 2.0, T)
    k = n((D, T)) / s / rk
    v = n((DV, T)) / (u * r)
    return {
        "qT": (n((B, D, NQ)) * s * (0.80 / np.sqrt(D))).astype(np.float32),
        "kT": k.astype(np.float32),
        "vT": v.astype(np.float32),
        "ks": np.tile(rk, (128, 1)).astype(np.float32),
        "vs": np.tile(u * r, (128, 1)).astype(np.float32),
        "sink": (2.0 + 3.0 * n((B, NQ, 1))).astype(np.float32),
        "offs": striped(idx),
    }


def reference(qT, kT, vT, ks, vs, sink, offs):
    idx = unstriped(offs)
    k = f64(kT)
    v = f64(vT)
    pick = lambda x: x[:, idx].reshape(x.shape[0], B, N).transpose(1, 0, 2)
    q = f64(qT)
    score = mxq(q, 1, "e4m3").transpose(0, 2, 1) @ mxq(pick(k), 1, "e4m3")
    score = score * pick(f64(ks))[:, :1, :]
    m = np.maximum(score.max(-1, keepdims=True), f64(sink))
    p = np.exp(score - m)
    total = p.sum(-1, keepdims=True) + np.exp(f64(sink) - m)
    w = p * pick(f64(vs))[:, :1, :]
    y = mxq(w, 2, "e4m3") @ mxq(pick(v).transpose(0, 2, 1), 1, "e4m3")
    y = y / total
    return y

@@ -1,0 +1,166 @@
+from contextlib import ExitStack
+
+import concourse.mybir as mybir
+from concourse.masks import make_identity
+
+D, T, N, DV, NQ = 512, 4096, 1024, 256, 128
+P = 128
+PACK = 4
+HALF = 512
+
+F32 = mybir.dt.float32
+BF16 = mybir.dt.bfloat16
+U32 = mybir.dt.uint32
+U16 = mybir.dt.uint16
+U8 = mybir.dt.uint8
+FP8X4 = mybir.dt.float8_e4m3fn_x4
+MULT = mybir.AluOpType.mult
+MIN = mybir.AluOpType.min
+AX = mybir.AxisListType.X
+COPY = mybir.ActivationFunctionType.Copy
+EXP = mybir.ActivationFunctionType.Exp
+
+FLOPS = 2 * NQ * N * (D + DV)
+BYTES = 4 * (D * T + DV * T + D * NQ + 2 * T + NQ + NQ * DV) + 2 * 128 * 64
+
+
+def tile_attend_x_ks_sink_topk_kernel(tc, qT, kT, vT, ks, vs, sink, offs, out):
+    nc = tc.nc
+    with ExitStack() as ctx:
+        keep = ctx.enter_context(tc.tile_pool(name="keep", bufs=1))
+        psum = ctx.enter_context(tc.psum_pool(name="psum", bufs=2))
+
+        offsets = keep.tile([P, N // 16], U16, name="offsets")
+        nc.sync.dma_start(offsets[:], offs)
+
+        q_raw = keep.tile([P, PACK, NQ], F32, name="q_raw")
+        nc.scalar.dma_start(q_raw[:], qT.rearrange("b (p t) q -> p (b t) q", t=PACK))
+        sink_col = keep.tile([P, 1], F32, name="sink_col")
+        nc.scalar.dma_start(sink_col[:], sink.rearrange("b q o -> (b q) o"))
+
+        ks_row = keep.tile([P, T], F32, name="ks_row")
+        vs_row = keep.tile([P, T], F32, name="vs_row")
+        k_rows = kT.rearrange("(p t) n -> p t n", t=PACK)
+        k_raw = []
+        for t in range(PACK):
+            kt = keep.tile([P, T], F32, name="k_raw%d" % t)
+            if 1 <= t <= 2:
+                row, scales = ((ks_row, ks), (vs_row, vs))[t - 1]
+                eng = (nc.vector, nc.gpsimd)[t - 1]
+                eng.memset(row[:], 0.0)
+                eng.memset(kt[:, 0:8], 0.0)
+                nc.sync.dma_start(row[0:1, :], scales[0:1, :])
+            nc.sync.dma_start(kt[:], k_rows[:, t, :])
+            k_raw.append(kt)
+        v_raw = []
+        for j in range(DV // P):
+            vt = keep.tile([P, T], F32, name="v_raw%d" % j)
+            nc.sync.dma_start(vt[:], vT[j * P : (j + 1) * P, :])
+            v_raw.append(vt)
+
+        ident = keep.tile([P, P], F32, name="ident")
+        make_identity(nc, ident[:])
+        warm = keep.tile([P, 1], F32, name="warm")
+        nc.scalar.activation(warm[:], ident[:, 0:1], EXP)
+
+        q_bf = keep.tile([P, NQ, PACK], BF16, name="q_bf", align_bytes=64)
+        nc.scalar.copy(q_bf[:], q_raw[:].rearrange("p t q -> p q t"))
+        q_codes = keep.tile([P, NQ], U32, name="q_codes", align_bytes=64)
+        q_scales = keep.tile([P, NQ], U8, name="q_scales", align_bytes=64)
+        nc.vector.quantize_mx(q_codes[:].bitcast(FP8X4), q_scales[:], q_bf[:].rearrange("p q t -> p (q t)"))
+
+        a_neg = keep.tile([P, N + 2], F32, name="a_neg")
+        nc.vector.tensor_scalar(a_neg[:, N : N + 1], sink_col[:], -1.0, None, MULT)
+
+        ks_got = keep.tile([P, N], F32, name="ks_got")
+        nc.vector.tensor_copy(ks_got[:], ks_row[:].indirect(offsets[:]))
+        vs_got = keep.tile([P, N], F32, name="vs_got")
+        nc.vector.tensor_copy(vs_got[:], vs_row[:].indirect(offsets[:]))
+
+        ks_col = keep.tile([P, 8], F32, name="ks_col")
+        ks_neg = keep.tile([P, N], F32, name="ks_neg")
+        for h in range(2):
+            turned = psum.tile([P, 4, P], F32, name="wt")
+            for c in range(4):
+                at = h * HALF + c * P
+                nc.tensor.transpose(turned[:, c, :], ks_got[:, at : at + P], ident[:])
+            nc.vector.tensor_copy(ks_col[:, 4 * h : 4 * h + 4], turned[:, :, 0])
+        for h in range(2):
+            spread = psum.tile([P, 4, P], F32, name="sc")
+            for c in range(4):
+                nc.tensor.transpose(spread[:, c, :], ks_col[:, 4 * h + c : 4 * h + c + 1].to_broadcast([P, P]), ident[:])
+            nc.scalar.activation(ks_neg[:, h * HALF : (h + 1) * HALF], spread[:].rearrange("p c s -> p (c s)"), COPY, scale=-1.0)
+        vs_col = keep.tile([P, 8], F32, name="vs_col")
+        for g in range(2):
+            turned = psum.tile([P, 4, P], F32, name="wt")
+            for t in range(PACK):
+                nc.tensor.transpose(turned[:, t, :], vs_got[:, g * HALF + t : (g + 1) * HALF : PACK], ident[:])
+            nc.vector.tensor_copy(vs_col[:, 4 * g : 4 * g + 4], turned[:, :, 0])
+
+        k_bf = keep.tile([P, N, PACK], BF16, name="k_bf", align_bytes=64)
+        k_codes = keep.tile([P, N], U32, name="k_codes", align_bytes=64)
+        k_scales = keep.tile([P, N], U8, name="k_scales", align_bytes=64)
+        for t in range(PACK - 1):
+            nc.vector.tensor_copy(k_bf[:, :, t], k_raw[t][:].indirect(offsets[:]))
+        scores = []
+        for h in range(2):
+            s = slice(h * HALF, (h + 1) * HALF)
+            nc.vector.tensor_copy(k_bf[:, s, PACK - 1], k_raw[PACK - 1][:].indirect(offsets[:, h * 32 : (h + 1) * 32]))
+            nc.vector.quantize_mx(k_codes[:, s].bitcast(FP8X4), k_scales[:, s], k_bf[:, s, :].rearrange("p n t -> p (n t)"))
+            sc = psum.tile([P, HALF], F32, name="sc")
+            nc.tensor.matmul_mx(sc[:], lhsT=q_codes[:].bitcast(FP8X4), lhsT_scale=q_scales[:],
+                                rhs=k_codes[:, s].bitcast(FP8X4), rhs_scale=k_scales[:, s], start=True, stop=True)
+            scores.append(sc)
+
+        m_neg = keep.tile([P, 1], F32, name="m_neg")
+        for h in range(2):
+            s = slice(h * HALF, (h + 1) * HALF)
+            nc.vector.tensor_tensor(a_neg[:, s], scores[h][:], ks_neg[:, s], MULT)
+            if h == 0:
+                nc.vector.tensor_reduce(a_neg[:, N + 1 : N + 2], a_neg[:, s], AX, MIN)
+            else:
+                nc.vector.tensor_reduce(m_neg[:], a_neg[:, HALF : N + 2], AX, MIN)
+        p = keep.tile([P, 2, PACK, P], F32, name="p")
+        sums = keep.tile([P, 3], F32, name="sums")
+        for g in range(2):
+            nc.scalar.activation(p[:, g].rearrange("q t s -> q s t"),
+                                 a_neg[:, g * HALF : (g + 1) * HALF].rearrange("q (s t) -> q s t", t=PACK),
+                                 EXP, bias=m_neg[:], scale=-1.0, accum_out=sums[:, g : g + 1])
+        nc.scalar.activation(sums[:, 2:3], sink_col[:], EXP, bias=m_neg[:])
+
+        w_bf = keep.tile([P, 2, NQ, PACK], BF16, name="w_bf", align_bytes=64)
+        w_codes = keep.tile([P, 2, NQ], U32, name="w_codes", align_bytes=64)
+        w_scales = keep.tile([P, 2, NQ], U8, name="w_scales", align_bytes=64)
+        for g in range(2):
+            turned = psum.tile([P, PACK, NQ], F32, name="wt")
+            for t in range(PACK):
+                nc.tensor.transpose(turned[:, t, :], p[:, g, t, :], ident[:])
+            nc.vector.tensor_tensor(w_bf[:, g], turned[:].rearrange("s t q -> s q t"),
+                                    vs_col[:, 4 * g : 4 * g + 4].unsqueeze(1).to_broadcast([P, NQ, PACK]), MULT)
+        nc.vector.quantize_mx(w_codes[:].rearrange("p g q -> p (g q)").bitcast(FP8X4), w_scales[:].rearrange("p g q -> p (g q)"),
+                              w_bf[:].rearrange("p g q t -> p (g q t)"))
+        total = keep.tile([P, 1], F32, name="total")
+        nc.vector.tensor_reduce(total[:], sums[:], AX, mybir.AluOpType.add)
+        inv = keep.tile([P, 1], F32, name="inv")
+        nc.vector.reciprocal(inv[:], total[:])
+
+        y_out = out.rearrange("b q e -> (b q) e")
+        for j in range(DV // P):
+            v_got = keep.tile([P, N], F32, name="v_got%d" % j)
+            v_bf = keep.tile([P, 2, P, PACK], BF16, name="v_bf%d" % j, align_bytes=64)
+            v_codes = keep.tile([P, 2, P], U32, name="v_codes%d" % j, align_bytes=64)
+            v_scales = keep.tile([P, 2, P], U8, name="v_scales%d" % j, align_bytes=64)
+            for g in range(2):
+                nc.vector.tensor_copy(v_got[:, g * HALF : (g + 1) * HALF], v_raw[j][:].indirect(offsets[:, g * 32 : (g + 1) * 32]))
+                turned = psum.tile([P, PACK, P], F32, name="vt")
+                for t in range(PACK):
+                    nc.tensor.transpose(turned[:, t, :], v_got[:, g * HALF + t : (g + 1) * HALF : PACK], ident[:])
+                nc.scalar.copy(v_bf[:, g], turned[:].rearrange("s t e -> s e t"))
+                nc.vector.quantize_mx(v_codes[:, g].bitcast(FP8X4), v_scales[:, g], v_bf[:, g].rearrange("p e t -> p (e t)"))
+            acc = psum.tile([P, P], F32, name="acc")
+            for g in range(2):
+                nc.tensor.matmul_mx(acc[:], lhsT=w_codes[:, g].bitcast(FP8X4), lhsT_scale=w_scales[:, g],
+                                    rhs=v_codes[:, g].bitcast(FP8X4), rhs_scale=v_scales[:, g], start=(g == 0), stop=(g == 1))
+            y = keep.tile([P, P], F32, name="y%d" % j)
+            nc.scalar.activation(y[:], acc[:], COPY, scale=inv[:])
+            nc.sync.dma_start(y_out[:, j * P : (j + 1) * P], y[:])

@@ -34,32 +34,34 @@ def tile_attend_x_ks_sink_topk_kernel(tc, qT, kT, vT, ks, vs, sink, offs, out):
         nc.sync.dma_start(offsets[:], offs)
 
         q_raw = keep.tile([P, PACK, NQ], F32, name="q_raw")
-        nc.scalar.dma_start(q_raw[:], qT.rearrange("b (p t) q -> p (b t) q", t=PACK))
         sink_col = keep.tile([P, 1], F32, name="sink_col")
         nc.scalar.dma_start(sink_col[:], sink.rearrange("b q o -> (b q) o"))
 
         ks_row = keep.tile([P, T], F32, name="ks_row")
         vs_row = keep.tile([P, T], F32, name="vs_row")
         k_rows = kT.rearrange("(p t) n -> p t n", t=PACK)
-        k_raw = []
-        for t in range(PACK):
-            kt = keep.tile([P, T], F32, name="k_raw%d" % t)
-            if 1 <= t <= 2:
-                row, scales = ((ks_row, ks), (vs_row, vs))[t - 1]
-                eng = (nc.vector, nc.gpsimd)[t - 1]
-                eng.memset(row[:], 0.0)
-                eng.memset(kt[:, 0:8], 0.0)
-                nc.sync.dma_start(row[0:1, :], scales[0:1, :])
-            nc.sync.dma_start(kt[:], k_rows[:, t, :])
-            k_raw.append(kt)
-        v_raw = []
+        k_raw = [keep.tile([P, T], F32, name="k_raw%d" % t) for t in range(PACK)]
+        v_raw = [keep.tile([P, T], F32, name="v_raw%d" % j) for j in range(DV // P)]
+        nc.sync.dma_start(k_raw[0][:], k_rows[:, 0, :])
+        nc.vector.memset(ks_row[:], 0.0)
+        nc.scalar.dma_start(ks_row[0:1, :], ks[0:1, :])
+        nc.vector.memset(k_raw[1][:, 0:8], 0.0)
+        nc.sync.dma_start(k_raw[1][:], k_rows[:, 1, :])
+        nc.vector.memset(vs_row[:], 0.0)
+        nc.scalar.dma_start(vs_row[0:1, :], vs[0:1, :])
+        for t in range(2, PACK):
+            nc.vector.memset(k_raw[t][:, 0:8], 0.0)
+            nc.sync.dma_start(k_raw[t][:], k_rows[:, t, :])
+        nc.vector.memset(q_raw[:, 0, 0:8], 0.0)
+        nc.sync.dma_start(q_raw[:], qT.rearrange("b (p t) q -> p (b t) q", t=PACK))
         for j in range(DV // P):
-            vt = keep.tile([P, T], F32, name="v_raw%d" % j)
-            nc.sync.dma_start(vt[:], vT[j * P : (j + 1) * P, :])
-            v_raw.append(vt)
+            nc.vector.memset(v_raw[j][:, 0:8], 0.0)
+            nc.sync.dma_start(v_raw[j][:], vT[j * P : (j + 1) * P, :])
 
         ident = keep.tile([P, P], F32, name="ident")
         make_identity(nc, ident[:])
+        ident_bf = keep.tile([P, P], BF16, name="ident_bf")
+        make_identity(nc, ident_bf[:])
         warm = keep.tile([P, 1], F32, name="warm")
         nc.scalar.activation(warm[:], ident[:, 0:1], EXP)
 
@@ -112,6 +114,11 @@ def tile_attend_x_ks_sink_topk_kernel(tc, qT, kT, vT, ks, vs, sink, offs, out):
                                 rhs=k_codes[:, s].bitcast(FP8X4), rhs_scale=k_scales[:, s], start=True, stop=True)
             scores.append(sc)
 
+        v_got = [keep.tile([P, 2, PACK, P], BF16, name="v_got%d" % j) for j in range(DV // P)]
+        for j in range(DV // P):
+            for g in range(2):
+                nc.vector.tensor_copy(v_got[j][:, g].rearrange("e t s -> e s t"), v_raw[j][:].indirect(offsets[:, g * 32 : (g + 1) * 32]))
+
         m_neg = keep.tile([P, 1], F32, name="m_neg")
         for h in range(2):
             s = slice(h * HALF, (h + 1) * HALF)
@@ -146,15 +153,13 @@ def tile_attend_x_ks_sink_topk_kernel(tc, qT, kT, vT, ks, vs, sink, offs, out):
 
         y_out = out.rearrange("b q e -> (b q) e")
         for j in range(DV // P):
-            v_got = keep.tile([P, N], F32, name="v_got%d" % j)
             v_bf = keep.tile([P, 2, P, PACK], BF16, name="v_bf%d" % j, align_bytes=64)
             v_codes = keep.tile([P, 2, P], U32, name="v_codes%d" % j, align_bytes=64)
             v_scales = keep.tile([P, 2, P], U8, name="v_scales%d" % j, align_bytes=64)
             for g in range(2):
-                nc.vector.tensor_copy(v_got[:, g * HALF : (g + 1) * HALF], v_raw[j][:].indirect(offsets[:, g * 32 : (g + 1) * 32]))
-                turned = psum.tile([P, PACK, P], F32, name="vt")
+                turned = psum.tile([P, PACK, P], BF16, name="vt")
                 for t in range(PACK):
-                    nc.tensor.transpose(turned[:, t, :], v_got[:, g * HALF + t : (g + 1) * HALF : PACK], ident[:])
+                    nc.tensor.transpose(turned[:, t, :], v_got[j][:, g, t, :], ident_bf[:])
                 nc.scalar.copy(v_bf[:, g], turned[:].rearrange("s t e -> s e t"))
                 nc.vector.quantize_mx(v_codes[:, g].bitcast(FP8X4), v_scales[:, g], v_bf[:, g].rearrange("p e t -> p (e t)"))
             acc = psum.tile([P, P], F32, name="acc")

@@ -41,16 +41,16 @@ def tile_attend_x_ks_sink_topk_kernel(tc, qT, kT, vT, ks, vs, sink, offs, out):
         vs_row = keep.tile([P, T], F32, name="vs_row")
         k_rows = kT.rearrange("(p t) n -> p t n", t=PACK)
         k_raw = [keep.tile([P, T], F32, name="k_raw%d" % t) for t in range(PACK)]
-        v_raw = [keep.tile([P, T], F32, name="v_raw%d" % j) for j in range(DV // P)]
+        v_raw = [keep.tile([P, T], F32, name="v_raw%d" % j, tag="v_raw%d" % j, align_bytes=64) for j in range(DV // P)]
         nc.sync.dma_start(k_raw[0][:], k_rows[:, 0, :])
         nc.vector.memset(ks_row[:], 0.0)
         nc.scalar.dma_start(ks_row[0:1, :], ks[0:1, :])
-        nc.vector.memset(k_raw[1][:, 0:8], 0.0)
+        nc.vector.memset(k_raw[1][:, 0:256], 0.0)
         nc.sync.dma_start(k_raw[1][:], k_rows[:, 1, :])
         nc.vector.memset(vs_row[:], 0.0)
         nc.scalar.dma_start(vs_row[0:1, :], vs[0:1, :])
         for t in range(2, PACK):
-            nc.vector.memset(k_raw[t][:, 0:8], 0.0)
+            nc.vector.memset(k_raw[t][:, 0:256], 0.0)
             nc.sync.dma_start(k_raw[t][:], k_rows[:, t, :])
         nc.vector.memset(q_raw[:, 0, 0:8], 0.0)
         nc.sync.dma_start(q_raw[:], qT.rearrange("b (p t) q -> p (b t) q", t=PACK))
@@ -60,8 +60,6 @@ def tile_attend_x_ks_sink_topk_kernel(tc, qT, kT, vT, ks, vs, sink, offs, out):
 
         ident = keep.tile([P, P], F32, name="ident")
         make_identity(nc, ident[:])
-        ident_bf = keep.tile([P, P], BF16, name="ident_bf")
-        make_identity(nc, ident_bf[:])
         warm = keep.tile([P, 1], F32, name="warm")
         nc.scalar.activation(warm[:], ident[:, 0:1], EXP)
 
@@ -102,8 +100,11 @@ def tile_attend_x_ks_sink_topk_kernel(tc, qT, kT, vT, ks, vs, sink, offs, out):
         k_bf = keep.tile([P, N, PACK], BF16, name="k_bf", align_bytes=64)
         k_codes = keep.tile([P, N], U32, name="k_codes", align_bytes=64)
         k_scales = keep.tile([P, N], U8, name="k_scales", align_bytes=64)
-        for t in range(PACK - 1):
-            nc.vector.tensor_copy(k_bf[:, :, t], k_raw[t][:].indirect(offsets[:]))
+        k_got = keep.tile([P, 2, N], F32, name="k_got")
+        for t in range(2):
+            nc.vector.tensor_copy(k_got[:, t, :], k_raw[t][:].indirect(offsets[:]))
+        nc.scalar.copy(k_bf[:, :, 0:2], k_got[:].rearrange("p t n -> p n t"))
+        nc.vector.tensor_copy(k_bf[:, :, 2], k_raw[2][:].indirect(offsets[:]))
         scores = []
         for h in range(2):
             s = slice(h * HALF, (h + 1) * HALF)
@@ -114,10 +115,10 @@ def tile_attend_x_ks_sink_topk_kernel(tc, qT, kT, vT, ks, vs, sink, offs, out):
                                 rhs=k_codes[:, s].bitcast(FP8X4), rhs_scale=k_scales[:, s], start=True, stop=True)
             scores.append(sc)
 
-        v_got = [keep.tile([P, 2, PACK, P], BF16, name="v_got%d" % j) for j in range(DV // P)]
+        v_got = [keep.tile([P, N], F32, name="v_got%d" % j) for j in range(DV // P)]
         for j in range(DV // P):
             for g in range(2):
-                nc.vector.tensor_copy(v_got[j][:, g].rearrange("e t s -> e s t"), v_raw[j][:].indirect(offsets[:, g * 32 : (g + 1) * 32]))
+                nc.vector.tensor_copy(v_got[j][:, g * HALF : (g + 1) * HALF], v_raw[j][:].indirect(offsets[:, g * 32 : (g + 1) * 32]))
 
         m_neg = keep.tile([P, 1], F32, name="m_neg")
         for h in range(2):
@@ -135,7 +136,7 @@ def tile_attend_x_ks_sink_topk_kernel(tc, qT, kT, vT, ks, vs, sink, offs, out):
                                  EXP, bias=m_neg[:], scale=-1.0, accum_out=sums[:, g : g + 1])
         nc.scalar.activation(sums[:, 2:3], sink_col[:], EXP, bias=m_neg[:])
 
-        w_bf = keep.tile([P, 2, NQ, PACK], BF16, name="w_bf", align_bytes=64)
+        w_bf = keep.tile([P, 2, NQ, PACK], BF16, name="w_bf", tag="v_raw1", align_bytes=64)
         w_codes = keep.tile([P, 2, NQ], U32, name="w_codes", align_bytes=64)
         w_scales = keep.tile([P, 2, NQ], U8, name="w_scales", align_bytes=64)
         for g in range(2):
@@ -151,21 +152,24 @@ def tile_attend_x_ks_sink_topk_kernel(tc, qT, kT, vT, ks, vs, sink, offs, out):
         inv = keep.tile([P, 1], F32, name="inv")
         nc.vector.reciprocal(inv[:], total[:])
 
+        v_bf = [keep.tile([P, 2, P, PACK], BF16, name="v_bf%d" % j, align_bytes=64) for j in range(DV // P)]
+        v_codes = [keep.tile([P, 2, P], U32, name="v_codes%d" % j, align_bytes=64) for j in range(DV // P)]
+        v_scales = [keep.tile([P, 2, P], U8, name="v_scales%d" % j, align_bytes=64) for j in range(DV // P)]
+        for j in range(DV // P):
+            for g in range(2):
+                turned = psum.tile([P, PACK, P], F32, name=("vt", "sc")[j])
+                for t in range(PACK):
+                    nc.tensor.transpose(turned[:, t, :], v_got[j][:, g * HALF + t : (g + 1) * HALF : PACK], ident[:])
+                nc.scalar.copy(v_bf[j][:, g], turned[:].rearrange("s t e -> s e t"))
+        for j in range(DV // P):
+            for g in range(2):
+                nc.vector.quantize_mx(v_codes[j][:, g].bitcast(FP8X4), v_scales[j][:, g], v_bf[j][:, g].rearrange("p e t -> p (e t)"))
         y_out = out.rearrange("b q e -> (b q) e")
         for j in range(DV // P):
-            v_bf = keep.tile([P, 2, P, PACK], BF16, name="v_bf%d" % j, align_bytes=64)
-            v_codes = keep.tile([P, 2, P], U32, name="v_codes%d" % j, align_bytes=64)
-            v_scales = keep.tile([P, 2, P], U8, name="v_scales%d" % j, align_bytes=64)
-            for g in range(2):
-                turned = psum.tile([P, PACK, P], BF16, name="vt")
-                for t in range(PACK):
-                    nc.tensor.transpose(turned[:, t, :], v_got[j][:, g, t, :], ident_bf[:])
-                nc.scalar.copy(v_bf[:, g], turned[:].rearrange("s t e -> s e t"))
-                nc.vector.quantize_mx(v_codes[:, g].bitcast(FP8X4), v_scales[:, g], v_bf[:, g].rearrange("p e t -> p (e t)"))
             acc = psum.tile([P, P], F32, name="acc")
             for g in range(2):
                 nc.tensor.matmul_mx(acc[:], lhsT=w_codes[:, g].bitcast(FP8X4), lhsT_scale=w_scales[:, g],
-                                    rhs=v_codes[:, g].bitcast(FP8X4), rhs_scale=v_scales[:, g], start=(g == 0), stop=(g == 1))
+                                    rhs=v_codes[j][:, g].bitcast(FP8X4), rhs_scale=v_scales[j][:, g], start=(g == 0), stop=(g == 1))
             y = keep.tile([P, P], F32, name="y%d" % j)
             nc.scalar.activation(y[:], acc[:], COPY, scale=inv[:])
             nc.sync.dma_start(y_out[:, j * P : (j + 1) * P], y[:])

@@ -34,6 +34,7 @@ def tile_attend_x_ks_sink_topk_kernel(tc, qT, kT, vT, ks, vs, sink, offs, out):
         nc.sync.dma_start(offsets[:], offs)
 
         q_raw = keep.tile([P, PACK, NQ], F32, name="q_raw")
+        nc.sync.dma_start(q_raw[:], qT.rearrange("b (p t) q -> p (b t) q", t=PACK))
         sink_col = keep.tile([P, 1], F32, name="sink_col")
         nc.scalar.dma_start(sink_col[:], sink.rearrange("b q o -> (b q) o"))
 
@@ -52,8 +53,6 @@ def tile_attend_x_ks_sink_topk_kernel(tc, qT, kT, vT, ks, vs, sink, offs, out):
         for t in range(2, PACK):
             nc.vector.memset(k_raw[t][:, 0:256], 0.0)
             nc.sync.dma_start(k_raw[t][:], k_rows[:, t, :])
-        nc.vector.memset(q_raw[:, 0, 0:8], 0.0)
-        nc.sync.dma_start(q_raw[:], qT.rearrange("b (p t) q -> p (b t) q", t=PACK))
         for j in range(DV // P):
             nc.vector.memset(v_raw[j][:, 0:8], 0.0)
             nc.sync.dma_start(v_raw[j][:], vT[j * P : (j + 1) * P, :])
@@ -84,7 +83,7 @@ def tile_attend_x_ks_sink_topk_kernel(tc, qT, kT, vT, ks, vs, sink, offs, out):
             for c in range(4):
                 at = h * HALF + c * P
                 nc.tensor.transpose(turned[:, c, :], ks_got[:, at : at + P], ident[:])
-            nc.vector.tensor_copy(ks_col[:, 4 * h : 4 * h + 4], turned[:, :, 0])
+            nc.scalar.copy(ks_col[:, 4 * h : 4 * h + 4], turned[:, :, 0])
         for h in range(2):
             spread = psum.tile([P, 4, P], F32, name="sc")
             for c in range(4):
@@ -95,7 +94,7 @@ def tile_attend_x_ks_sink_topk_kernel(tc, qT, kT, vT, ks, vs, sink, offs, out):
             turned = psum.tile([P, 4, P], F32, name="wt")
             for t in range(PACK):
                 nc.tensor.transpose(turned[:, t, :], vs_got[:, g * HALF + t : (g + 1) * HALF : PACK], ident[:])
-            nc.vector.tensor_copy(vs_col[:, 4 * g : 4 * g + 4], turned[:, :, 0])
+            nc.scalar.copy(vs_col[:, 4 * g : 4 * g + 4], turned[:, :, 0])
 
         k_bf = keep.tile([P, N, PACK], BF16, name="k_bf", align_bytes=64)
         k_codes = keep.tile([P, N], U32, name="k_codes", align_bytes=64)
@@ -104,11 +103,14 @@ def tile_attend_x_ks_sink_topk_kernel(tc, qT, kT, vT, ks, vs, sink, offs, out):
         for t in range(2):
             nc.vector.tensor_copy(k_got[:, t, :], k_raw[t][:].indirect(offsets[:]))
         nc.scalar.copy(k_bf[:, :, 0:2], k_got[:].rearrange("p t n -> p n t"))
-        nc.vector.tensor_copy(k_bf[:, :, 2], k_raw[2][:].indirect(offsets[:]))
+        k_late = keep.tile([P, 2, HALF], F32, name="k_late")
+        for t in range(2, PACK):
+            nc.vector.tensor_copy(k_late[:, t - 2, :], k_raw[t][:].indirect(offsets[:, 32:64]))
+            nc.vector.tensor_copy(k_bf[:, 0:HALF, t], k_raw[t][:].indirect(offsets[:, 0:32]))
+        nc.scalar.copy(k_bf[:, HALF:N, 2:4], k_late[:].rearrange("p t n -> p n t"))
         scores = []
         for h in range(2):
             s = slice(h * HALF, (h + 1) * HALF)
-            nc.vector.tensor_copy(k_bf[:, s, PACK - 1], k_raw[PACK - 1][:].indirect(offsets[:, h * 32 : (h + 1) * 32]))
             nc.vector.quantize_mx(k_codes[:, s].bitcast(FP8X4), k_scales[:, s], k_bf[:, s, :].rearrange("p n t -> p (n t)"))
             sc = psum.tile([P, HALF], F32, name="sc")
             nc.tensor.matmul_mx(sc[:], lhsT=q_codes[:].bitcast(FP8X4), lhsT_scale=q_scales[:],
@@ -153,7 +155,7 @@ def tile_attend_x_ks_sink_topk_kernel(tc, qT, kT, vT, ks, vs, sink, offs, out):
         nc.vector.reciprocal(inv[:], total[:])
 
         v_bf = [keep.tile([P, 2, P, PACK], BF16, name="v_bf%d" % j, align_bytes=64) for j in range(DV // P)]
-        v_codes = [keep.tile([P, 2, P], U32, name="v_codes%d" % j, align_bytes=64) for j in range(DV // P)]
+        v_codes = keep.tile([P, DV // P, 2, P], U32, name="v_codes", tag="v_raw1", align_bytes=64)
         v_scales = [keep.tile([P, 2, P], U8, name="v_scales%d" % j, align_bytes=64) for j in range(DV // P)]
         for j in range(DV // P):
             for g in range(2):
@@ -163,13 +165,13 @@ def tile_attend_x_ks_sink_topk_kernel(tc, qT, kT, vT, ks, vs, sink, offs, out):
                 nc.scalar.copy(v_bf[j][:, g], turned[:].rearrange("s t e -> s e t"))
         for j in range(DV // P):
             for g in range(2):
-                nc.vector.quantize_mx(v_codes[j][:, g].bitcast(FP8X4), v_scales[j][:, g], v_bf[j][:, g].rearrange("p e t -> p (e t)"))
+                nc.vector.quantize_mx(v_codes[:, j, g].bitcast(FP8X4), v_scales[j][:, g], v_bf[j][:, g].rearrange("p e t -> p (e t)"))
         y_out = out.rearrange("b q e -> (b q) e")
         for j in range(DV // P):
             acc = psum.tile([P, P], F32, name="acc")
             for g in range(2):
                 nc.tensor.matmul_mx(acc[:], lhsT=w_codes[:, g].bitcast(FP8X4), lhsT_scale=w_scales[:, g],
-                                    rhs=v_codes[j][:, g].bitcast(FP8X4), rhs_scale=v_scales[j][:, g], start=(g == 0), stop=(g == 1))
+                                    rhs=v_codes[:, j, g].bitcast(FP8X4), rhs_scale=v_scales[j][:, g], start=(g == 0), stop=(g == 1))
             y = keep.tile([P, P], F32, name="y%d" % j)
             nc.scalar.activation(y[:], acc[:], COPY, scale=inv[:])
             nc.sync.dma_start(y_out[:, j * P : (j + 1) * P], y[:])

from contextlib import ExitStack

import concourse.mybir as mybir
from concourse.masks import make_identity

D, T, N, DV, NQ = 512, 4096, 1024, 256, 128
P = 128
PACK = 4
HALF = 512

F32 = mybir.dt.float32
BF16 = mybir.dt.bfloat16
U32 = mybir.dt.uint32
U16 = mybir.dt.uint16
U8 = mybir.dt.uint8
FP8X4 = mybir.dt.float8_e4m3fn_x4
MULT = mybir.AluOpType.mult
MIN = mybir.AluOpType.min
AX = mybir.AxisListType.X
COPY = mybir.ActivationFunctionType.Copy
EXP = mybir.ActivationFunctionType.Exp

FLOPS = 2 * NQ * N * (D + DV)
BYTES = 4 * (D * T + DV * T + D * NQ + 2 * T + NQ + NQ * DV) + 2 * 128 * 64


def tile_attend_x_ks_sink_topk_kernel(tc, qT, kT, vT, ks, vs, sink, offs, out):
    nc = tc.nc
    with ExitStack() as ctx:
        keep = ctx.enter_context(tc.tile_pool(name="keep", bufs=1))
        psum = ctx.enter_context(tc.psum_pool(name="psum", bufs=2))

        offsets = keep.tile([P, N // 16], U16, name="offsets")
        nc.sync.dma_start(offsets[:], offs)

        q_raw = keep.tile([P, PACK, NQ], F32, name="q_raw")
        nc.sync.dma_start(q_raw[:], qT.rearrange("b (p t) q -> p (b t) q", t=PACK))
        sink_col = keep.tile([P, 1], F32, name="sink_col")
        nc.scalar.dma_start(sink_col[:], sink.rearrange("b q o -> (b q) o"))

        ks_row = keep.tile([P, T], F32, name="ks_row")
        vs_row = keep.tile([P, T], F32, name="vs_row")
        k_rows = kT.rearrange("(p t) n -> p t n", t=PACK)
        k_raw = [keep.tile([P, T], F32, name="k_raw%d" % t) for t in range(PACK)]
        v_raw = [keep.tile([P, T], F32, name="v_raw%d" % j, tag="v_raw%d" % j, align_bytes=64) for j in range(DV // P)]
        nc.sync.dma_start(k_raw[0][:], k_rows[:, 0, :])
        nc.vector.memset(ks_row[:], 0.0)
        nc.scalar.dma_start(ks_row[0:1, :], ks[0:1, :])
        nc.vector.memset(k_raw[1][:, 0:256], 0.0)
        nc.sync.dma_start(k_raw[1][:], k_rows[:, 1, :])
        nc.vector.memset(vs_row[:], 0.0)
        nc.scalar.dma_start(vs_row[0:1, :], vs[0:1, :])
        for t in range(2, PACK):
            nc.vector.memset(k_raw[t][:, 0:256], 0.0)
            nc.sync.dma_start(k_raw[t][:], k_rows[:, t, :])
        for j in range(DV // P):
            nc.vector.memset(v_raw[j][:, 0:8], 0.0)
            nc.sync.dma_start(v_raw[j][:], vT[j * P : (j + 1) * P, :])

        ident = keep.tile([P, P], F32, name="ident")
        make_identity(nc, ident[:])
        warm = keep.tile([P, 1], F32, name="warm")
        nc.scalar.activation(warm[:], ident[:, 0:1], EXP)

        q_bf = keep.tile([P, NQ, PACK], BF16, name="q_bf", align_bytes=64)
        nc.scalar.copy(q_bf[:], q_raw[:].rearrange("p t q -> p q t"))
        q_codes = keep.tile([P, NQ], U32, name="q_codes", align_bytes=64)
        q_scales = keep.tile([P, NQ], U8, name="q_scales", align_bytes=64)
        nc.vector.quantize_mx(q_codes[:].bitcast(FP8X4), q_scales[:], q_bf[:].rearrange("p q t -> p (q t)"))

        a_neg = keep.tile([P, N + 2], F32, name="a_neg")
        nc.vector.tensor_scalar(a_neg[:, N : N + 1], sink_col[:], -1.0, None, MULT)

        ks_got = keep.tile([P, N], F32, name="ks_got")
        nc.vector.tensor_copy(ks_got[:], ks_row[:].indirect(offsets[:]))
        vs_got = keep.tile([P, N], F32, name="vs_got")
        nc.vector.tensor_copy(vs_got[:], vs_row[:].indirect(offsets[:]))

        ks_col = keep.tile([P, 8], F32, name="ks_col")
        ks_neg = keep.tile([P, N], F32, name="ks_neg")
        for h in range(2):
            turned = psum.tile([P, 4, P], F32, name="wt")
            for c in range(4):
                at = h * HALF + c * P
                nc.tensor.transpose(turned[:, c, :], ks_got[:, at : at + P], ident[:])
            nc.scalar.copy(ks_col[:, 4 * h : 4 * h + 4], turned[:, :, 0])
        for h in range(2):
            spread = psum.tile([P, 4, P], F32, name="sc")
            for c in range(4):
                nc.tensor.transpose(spread[:, c, :], ks_col[:, 4 * h + c : 4 * h + c + 1].to_broadcast([P, P]), ident[:])
            nc.scalar.activation(ks_neg[:, h * HALF : (h + 1) * HALF], spread[:].rearrange("p c s -> p (c s)"), COPY, scale=-1.0)
        vs_col = keep.tile([P, 8], F32, name="vs_col")
        for g in range(2):
            turned = psum.tile([P, 4, P], F32, name="wt")
            for t in range(PACK):
                nc.tensor.transpose(turned[:, t, :], vs_got[:, g * HALF + t : (g + 1) * HALF : PACK], ident[:])
            nc.scalar.copy(vs_col[:, 4 * g : 4 * g + 4], turned[:, :, 0])

        k_bf = keep.tile([P, N, PACK], BF16, name="k_bf", align_bytes=64)
        k_codes = keep.tile([P, N], U32, name="k_codes", align_bytes=64)
        k_scales = keep.tile([P, N], U8, name="k_scales", align_bytes=64)
        k_got = keep.tile([P, 2, N], F32, name="k_got")
        for t in range(2):
            nc.vector.tensor_copy(k_got[:, t, :], k_raw[t][:].indirect(offsets[:]))
        nc.scalar.copy(k_bf[:, :, 0:2], k_got[:].rearrange("p t n -> p n t"))
        k_late = keep.tile([P, 2, HALF], F32, name="k_late")
        for t in range(2, PACK):
            nc.vector.tensor_copy(k_late[:, t - 2, :], k_raw[t][:].indirect(offsets[:, 32:64]))
            nc.vector.tensor_copy(k_bf[:, 0:HALF, t], k_raw[t][:].indirect(offsets[:, 0:32]))
        nc.scalar.copy(k_bf[:, HALF:N, 2:4], k_late[:].rearrange("p t n -> p n t"))
        scores = []
        for h in range(2):
            s = slice(h * HALF, (h + 1) * HALF)
            nc.vector.quantize_mx(k_codes[:, s].bitcast(FP8X4), k_scales[:, s], k_bf[:, s, :].rearrange("p n t -> p (n t)"))
            sc = psum.tile([P, HALF], F32, name="sc")
            nc.tensor.matmul_mx(sc[:], lhsT=q_codes[:].bitcast(FP8X4), lhsT_scale=q_scales[:],
                                rhs=k_codes[:, s].bitcast(FP8X4), rhs_scale=k_scales[:, s], start=True, stop=True)
            scores.append(sc)

        v_got = [keep.tile([P, N], F32, name="v_got%d" % j) for j in range(DV // P)]
        for j in range(DV // P):
            for g in range(2):
                nc.vector.tensor_copy(v_got[j][:, g * HALF : (g + 1) * HALF], v_raw[j][:].indirect(offsets[:, g * 32 : (g + 1) * 32]))

        m_neg = keep.tile([P, 1], F32, name="m_neg")
        for h in range(2):
            s = slice(h * HALF, (h + 1) * HALF)
            nc.vector.tensor_tensor(a_neg[:, s], scores[h][:], ks_neg[:, s], MULT)
            if h == 0:
                nc.vector.tensor_reduce(a_neg[:, N + 1 : N + 2], a_neg[:, s], AX, MIN)
            else:
                nc.vector.tensor_reduce(m_neg[:], a_neg[:, HALF : N + 2], AX, MIN)
        p = keep.tile([P, 2, PACK, P], F32, name="p")
        sums = keep.tile([P, 3], F32, name="sums")
        for g in range(2):
            nc.scalar.activation(p[:, g].rearrange("q t s -> q s t"),
                                 a_neg[:, g * HALF : (g + 1) * HALF].rearrange("q (s t) -> q s t", t=PACK),
                                 EXP, bias=m_neg[:], scale=-1.0, accum_out=sums[:, g : g + 1])
        nc.scalar.activation(sums[:, 2:3], sink_col[:], EXP, bias=m_neg[:])

        w_bf = keep.tile([P, 2, NQ, PACK], BF16, name="w_bf", tag="v_raw1", align_bytes=64)
        w_codes = keep.tile([P, 2, NQ], U32, name="w_codes", align_bytes=64)
        w_scales = keep.tile([P, 2, NQ], U8, name="w_scales", align_bytes=64)
        for g in range(2):
            turned = psum.tile([P, PACK, NQ], F32, name="wt")
            for t in range(PACK):
                nc.tensor.transpose(turned[:, t, :], p[:, g, t, :], ident[:])
            nc.vector.tensor_tensor(w_bf[:, g], turned[:].rearrange("s t q -> s q t"),
                                    vs_col[:, 4 * g : 4 * g + 4].unsqueeze(1).to_broadcast([P, NQ, PACK]), MULT)
        nc.vector.quantize_mx(w_codes[:].rearrange("p g q -> p (g q)").bitcast(FP8X4), w_scales[:].rearrange("p g q -> p (g q)"),
                              w_bf[:].rearrange("p g q t -> p (g q t)"))
        total = keep.tile([P, 1], F32, name="total")
        nc.vector.tensor_reduce(total[:], sums[:], AX, mybir.AluOpType.add)
        inv = keep.tile([P, 1], F32, name="inv")
        nc.vector.reciprocal(inv[:], total[:])

        v_bf = [keep.tile([P, 2, P, PACK], BF16, name="v_bf%d" % j, align_bytes=64) for j in range(DV // P)]
        v_codes = keep.tile([P, DV // P, 2, P], U32, name="v_codes", tag="v_raw1", align_bytes=64)
        v_scales = [keep.tile([P, 2, P], U8, name="v_scales%d" % j, align_bytes=64) for j in range(DV // P)]
        for j in range(DV // P):
            for g in range(2):
                turned = psum.tile([P, PACK, P], F32, name=("vt", "sc")[j])
                for t in range(PACK):
                    nc.tensor.transpose(turned[:, t, :], v_got[j][:, g * HALF + t : (g + 1) * HALF : PACK], ident[:])
                nc.scalar.copy(v_bf[j][:, g], turned[:].rearrange("s t e -> s e t"))
        for j in range(DV // P):
            for g in range(2):
                nc.vector.quantize_mx(v_codes[:, j, g].bitcast(FP8X4), v_scales[j][:, g], v_bf[j][:, g].rearrange("p e t -> p (e t)"))
        y_out = out.rearrange("b q e -> (b q) e")
        for j in range(DV // P):
            acc = psum.tile([P, P], F32, name="acc")
            for g in range(2):
                nc.tensor.matmul_mx(acc[:], lhsT=w_codes[:, g].bitcast(FP8X4), lhsT_scale=w_scales[:, g],
                                    rhs=v_codes[:, j, g].bitcast(FP8X4), rhs_scale=v_scales[j][:, g], start=(g == 0), stop=(g == 1))
            y = keep.tile([P, P], F32, name="y%d" % j)
            nc.scalar.activation(y[:], acc[:], COPY, scale=inv[:])
            nc.sync.dma_start(y_out[:, j * P : (j + 1) * P], y[:])
